import numpy as np
import ml_dtypes


def mxq(x, axis, fmt="e4m3"):
    dtype, down = {"e4m3": (ml_dtypes.float8_e4m3fn, 7), "e5m2": (ml_dtypes.float8_e5m2, 14)}[fmt]
    v = np.moveaxis(np.asarray(x, np.float32).astype(ml_dtypes.bfloat16).astype(np.float64), axis, -1)
    blocks = v.reshape(v.shape[:-1] + (-1, 32))
    amax = np.abs(blocks).max(-1, keepdims=True)
    byte = np.maximum(np.where(amax > 0, np.frexp(amax)[1] - 1 + 127, 0) - down, 1)
    scale = np.exp2(byte - 127.0)
    codes = (blocks / scale).astype(np.float32).astype(dtype).astype(np.float64)
    return np.moveaxis((codes * scale).reshape(v.shape), -1, axis)


WIDE = False


def mx_kscale(k):
    if not WIDE:
        return np.ones(k)
    levels = np.array([10, -10, 5, -5, 0])
    if k % 512:
        return np.exp2(np.random.permutation(np.resize(levels, k // 32))).repeat(32)
    a = np.empty((k // 512, 16))
    for p in range(k // 512):
        a[p, :8] = np.random.permutation(np.resize(levels, 8))
        for g in range(8):
            far = levels[np.abs(levels - a[p, g]) >= 10]
            a[p, g + 8] = far[np.random.randint(len(far))]
    return np.exp2(a.ravel()).repeat(32)


def f64(x):
    return np.asarray(x).astype(np.float64)


def striped(idx):
    return np.tile(idx.reshape(-1, 16).T, (8, 1)).astype(np.uint16)


def unstriped(offs):
    return offs[:16].T.reshape(-1).astype(np.int64)


def pack_weight(w):
    k, n = w.shape
    w = f64(np.asarray(w, np.float32).astype(ml_dtypes.bfloat16)).reshape(k // 32, 32, n)
    amax = np.abs(w).max(1)
    byte = np.clip(np.where(amax > 0, np.frexp(amax)[1] - 1 + 127 - 7, 1), 1, 254)
    scaled = (w * np.exp2(127.0 - byte)[:, None, :]).reshape(k, n).astype(np.float32)
    words = np.ascontiguousarray(scaled.reshape(k // 512, 128, 4, n).transpose(0, 1, 3, 2)).astype(ml_dtypes.float8_e4m3fn).view(np.uint8)
    return words, np.ascontiguousarray(byte.astype(np.uint8).reshape(k // 512, 16, n))


def unpack_weight(words, scales):
    g, p, n, _ = words.shape
    vals = np.ascontiguousarray(words).view(ml_dtypes.float8_e4m3fn).astype(np.float64) * np.repeat(np.exp2(scales.astype(np.float64) - 127.0), 8, axis=1)[..., None]
    return vals.transpose(0, 1, 3, 2).reshape(g * 512, n)


K, T, S, V = 1024, 2048, 512, 512
P = 2 ** 7


def setup_inputs():
    n = np.random.standard_normal
    s = mx_kscale(K)[:, None]
    packed_xT = pack_weight(n((K, T)) * s)
    return {
        "x_words": packed_xT[0],
        "x_scales": packed_xT[1],
        "hT": (n((K, V)) / np.sqrt(K) / s).astype(np.float32),
        "prev": (np.random.uniform(0.0, 3.0, (V, S))).astype(np.float32),
        "jump": (np.tile(np.random.uniform(1.0, 1.4, S), (P, 1))).astype(np.float32),
        "offs": striped(np.random.permutation(T)[:S]),
    }


def reference(x_words, x_scales, hT, prev, jump, offs):
    hTq = mxq(f64(hT), 0, "e4m3")
    xq = unpack_weight(x_words, x_scales)[:, unstriped(offs)]
    cst = -0.3 * (hTq.T @ xq) + 1.0
    mn = f64(prev).min(axis=1, keepdims=True)
    lq = f64(prev) - mn
    iv = -1.0 * lq + 5.0
    side = np.maximum(np.pad(iv, ((0, 0), (1, 0)))[:, :S], np.pad(iv, ((0, 0), (0, 1)))[:, 1:])
    return cst + np.minimum(np.minimum(lq, -1.0 * side + 5.3), f64(jump)[:1])

@@ -1,0 +1,146 @@
+from contextlib import ExitStack
+
+import concourse.mybir as mybir
+
+K, T, S, V = 1024, 2048, 512, 512
+FLOPS = 2 * K * V * S
+
+F32 = mybir.dt.float32
+BF16 = mybir.dt.bfloat16
+I32 = mybir.dt.int32
+U32 = mybir.dt.uint32
+U16 = mybir.dt.uint16
+U8 = mybir.dt.uint8
+FP8X4 = mybir.dt.float8_e4m3fn_x4
+ALU = mybir.AluOpType
+COPY = mybir.ActivationFunctionType.Copy
+
+P = 128
+PACK = 4
+K_PASS = P * PACK
+PASSES = K // K_PASS
+TILES = V // P
+PAD = 8
+F32_MAX = 3.4028234663852886e38
+
+
+def tile_picked_ysgm_cost_p_kernel(tc, x_words, x_scales, hT, prev, jump, offs, out):
+    nc = tc.nc
+    with ExitStack() as ctx:
+        keep = ctx.enter_context(tc.tile_pool(name="keep", bufs=1))
+        psum = ctx.enter_context(tc.psum_pool(name="psum", bufs=1))
+
+        offsets = keep.tile([P, S // 16], U16, name="offsets")
+        scale_table = keep.tile([P, T], U8, name="scale_table", align_bytes=64)
+        prev_sb = [keep.tile([P, PAD + S + PAD], F32, name=f"prev{i}") for i in range(TILES)]
+        jump_sb = keep.tile([P, S], F32, name="jump_sb")
+        h_raw = [keep.tile([P, PACK, V], F32, name=f"h_raw{o}") for o in range(PASSES)]
+        word_table = [keep.tile([P, T], U32, name=f"word_table{o}", align_bytes=64) for o in range(PASSES)]
+
+        nc.vector.memset(scale_table[:].bitcast(I32), 0)
+        for i in range(TILES):
+            nc.vector.memset(prev_sb[i][:, PAD - 1 : PAD + S + 1 : S + 1], F32_MAX)
+
+        def load_h(o):
+            rows = hT[o * K_PASS : (o + 1) * K_PASS, :]
+            nc.sync.dma_start(out=h_raw[o][:], in_=rows.rearrange("(p j) w -> p j w", j=PACK))
+
+        for i in range(TILES):
+            nc.sync.dma_start(out=prev_sb[i][:, PAD : PAD + S], in_=prev[i * P : (i + 1) * P, :])
+        nc.sync.dma_start(out=jump_sb[:], in_=jump)
+        load_h(0)
+        nc.sync.dma_start(offsets[:], offs)
+        for q in range(4):
+            nc.sync.dma_start(
+                out=scale_table[32 * q : 32 * q + 4 * PASSES, :].bitcast(I32),
+                in_=x_scales[:, 4 * q : 4 * q + 4, :].bitcast(I32),
+            )
+        load_h(1)
+        for o in range(PASSES):
+            nc.sync.dma_start(
+                out=word_table[o][:].bitcast(I32),
+                in_=x_words[o].rearrange("p c r -> p (c r)").bitcast(I32),
+            )
+
+        prev1 = [keep.tile([P, S], F32, name=f"prev1_{i}") for i in range(TILES)]
+        for i in range(TILES):
+            nc.scalar.activation(prev1[i][:], prev_sb[i][:, PAD : PAD + S], COPY, bias=1.0)
+        jump1 = keep.tile([P, S], F32, name="jump1")
+        nc.scalar.activation(jump1[:], jump_sb[:], COPY, bias=1.0)
+        nc.gpsimd.tensor_scalar(jump1[:, 0 : S : S - 1], jump1[:, 0 : S : S - 1], 6.3, None, op0=ALU.min)
+
+        h_bf = [keep.tile([P, V, PACK], BF16, name=f"h_bf{o}", align_bytes=64) for o in range(PASSES)]
+        for o in range(PASSES):
+            nc.scalar.copy(
+                out=h_bf[o][:].rearrange("p (c i) t -> p c t i", i=4),
+                in_=h_raw[o][:].rearrange("p t (c i) -> p c t i", i=4),
+            )
+
+        near = [keep.tile([P, 2, S], F32, name=f"near{u}") for u in range(TILES // 2)]
+        least = [keep.tile([P, 2], F32, name=f"least{u}") for u in range(TILES // 2)]
+        best = [keep.tile([P, S], F32, name=f"best{i}") for i in range(TILES)]
+        path = [keep.tile([P, S], F32, name=f"path{i}") for i in range(TILES)]
+
+        def neighbours(i):
+            nc.vector.tensor_tensor(
+                near[i // 2][:, i % 2, :],
+                prev_sb[i][:, PAD - 1 : PAD - 1 + S],
+                prev_sb[i][:, PAD + 1 : PAD + 1 + S],
+                ALU.min,
+            )
+
+        def row_least(u):
+            view = near[u][:].rearrange("p e (c f) -> p e c f", f=4)[:, :, :, 1:3]
+            nc.vector.tensor_reduce(least[u][:], view, mybir.AxisListType.XY, ALU.min)
+
+        def stay_or_step(i):
+            nc.vector.scalar_tensor_tensor(
+                best[i][:], near[i // 2][:, i % 2, :], 1.3, prev1[i][:], ALU.add, ALU.min
+            )
+
+        def or_jump(i):
+            nc.vector.scalar_tensor_tensor(
+                path[i][:], best[i][:], least[i // 2][:, i % 2 : i % 2 + 1], jump1[:], ALU.subtract, ALU.min
+            )
+
+        for u in range(TILES // 2):
+            a, b = 2 * u, 2 * u + 1
+            neighbours(a)
+            neighbours(b)
+            stay_or_step(a)
+            row_least(u)
+            stay_or_step(b)
+            or_jump(a)
+            or_jump(b)
+
+        x_scale = keep.tile([P, S], U8, name="x_scale", align_bytes=64)
+        nc.vector.tensor_copy(x_scale[:], scale_table[:].indirect(offsets[:]))
+
+        h_codes = [keep.tile([P, V], U32, name=f"h_codes{o}", align_bytes=64) for o in range(PASSES)]
+        h_scale = [keep.tile([P, V], U8, name=f"h_scale{o}", align_bytes=64) for o in range(PASSES)]
+        x_codes = [keep.tile([P, S], U32, name=f"x_codes{o}", align_bytes=64) for o in range(PASSES)]
+        acc = [psum.tile([P, S], F32, name=f"acc{i}") for i in range(TILES)]
+        for o in range(PASSES):
+            nc.vector.quantize_mx(
+                out=h_codes[o][:].bitcast(FP8X4),
+                scales=h_scale[o][:],
+                in_=h_bf[o][:].rearrange("p w j -> p (w j)"),
+            )
+        for o in range(PASSES):
+            nc.vector.tensor_copy(x_codes[o][:], word_table[o][:].indirect(offsets[:]))
+            for i in range(TILES):
+                cols = slice(i * P, (i + 1) * P)
+                nc.tensor.matmul_mx(
+                    out=acc[i][:],
+                    lhsT=h_codes[o][:, cols].bitcast(FP8X4),
+                    lhsT_scale=h_scale[o][:, cols],
+                    rhs=x_codes[o][:].bitcast(FP8X4),
+                    rhs_scale=x_scale[4 * o : P, :],
+                    start=(o == 0),
+                    stop=(o == PASSES - 1),
+                )
+
+        for i in range(TILES):
+            result = keep.tile([P, S], F32, name=f"result{i}")
+            nc.vector.scalar_tensor_tensor(result[:], acc[i][:], -0.3, path[i][:], ALU.mult, ALU.add)
+            nc.sync.dma_start(out=out[i * P : (i + 1) * P, :], in_=result[:])

@@ -35,11 +35,12 @@ def tile_picked_ysgm_cost_p_kernel(tc, x_words, x_scales, hT, prev, jump, offs, 
         prev_sb = [keep.tile([P, PAD + S + PAD], F32, name=f"prev{i}") for i in range(TILES)]
         jump_sb = keep.tile([P, S], F32, name="jump_sb")
         h_raw = [keep.tile([P, PACK, V], F32, name=f"h_raw{o}") for o in range(PASSES)]
-        word_table = [keep.tile([P, T], U32, name=f"word_table{o}", align_bytes=64) for o in range(PASSES)]
+        word_table = [keep.tile([P, T], U32, name=f"word_table{o}", tag=f"late{o}", align_bytes=64) for o in range(PASSES)]
 
         nc.vector.memset(scale_table[:].bitcast(I32), 0)
         for i in range(TILES):
-            nc.vector.memset(prev_sb[i][:, PAD - 1 : PAD + S + 1 : S + 1], F32_MAX)
+            nc.gpsimd.memset(prev_sb[i][:, 0:PAD], F32_MAX)
+            nc.gpsimd.memset(prev_sb[i][:, PAD + S :], F32_MAX)
 
         def load_h(o):
             rows = hT[o * K_PASS : (o + 1) * K_PASS, :]
@@ -69,7 +70,7 @@ def tile_picked_ysgm_cost_p_kernel(tc, x_words, x_scales, hT, prev, jump, offs, 
         nc.scalar.activation(jump1[:], jump_sb[:], COPY, bias=1.0)
         nc.gpsimd.tensor_scalar(jump1[:, 0 : S : S - 1], jump1[:, 0 : S : S - 1], 6.3, None, op0=ALU.min)
 
-        h_bf = [keep.tile([P, V, PACK], BF16, name=f"h_bf{o}", align_bytes=64) for o in range(PASSES)]
+        h_bf = [keep.tile([P, V, PACK], BF16, name=f"h_bf{o}", tag=f"h_bf{o}", align_bytes=64) for o in range(PASSES)]
         for o in range(PASSES):
             nc.scalar.copy(
                 out=h_bf[o][:].rearrange("p (c i) t -> p c t i", i=4),
@@ -79,7 +80,7 @@ def tile_picked_ysgm_cost_p_kernel(tc, x_words, x_scales, hT, prev, jump, offs, 
         near = [keep.tile([P, 2, S], F32, name=f"near{u}") for u in range(TILES // 2)]
         least = [keep.tile([P, 2], F32, name=f"least{u}") for u in range(TILES // 2)]
         best = [keep.tile([P, S], F32, name=f"best{i}") for i in range(TILES)]
-        path = [keep.tile([P, S], F32, name=f"path{i}") for i in range(TILES)]
+        path = {}
 
         def neighbours(i):
             nc.vector.tensor_tensor(
@@ -98,7 +99,8 @@ def tile_picked_ysgm_cost_p_kernel(tc, x_words, x_scales, hT, prev, jump, offs, 
                 best[i][:], near[i // 2][:, i % 2, :], 1.3, prev1[i][:], ALU.add, ALU.min
             )
 
-        def or_jump(i):
+        def or_jump(i, tag):
+            path[i] = keep.tile([P, S], F32, name=f"path{i}", tag=tag, align_bytes=64)
             nc.vector.scalar_tensor_tensor(
                 path[i][:], best[i][:], least[i // 2][:, i % 2 : i % 2 + 1], jump1[:], ALU.subtract, ALU.min
             )
@@ -110,24 +112,30 @@ def tile_picked_ysgm_cost_p_kernel(tc, x_words, x_scales, hT, prev, jump, offs, 
             stay_or_step(a)
             row_least(u)
             stay_or_step(b)
-            or_jump(a)
-            or_jump(b)
+            if u == 0:
+                or_jump(a, "path0")
+                or_jump(b, "path1")
 
         x_scale = keep.tile([P, S], U8, name="x_scale", align_bytes=64)
         nc.vector.tensor_copy(x_scale[:], scale_table[:].indirect(offsets[:]))
 
-        h_codes = [keep.tile([P, V], U32, name=f"h_codes{o}", align_bytes=64) for o in range(PASSES)]
+        h_codes = {}
         h_scale = [keep.tile([P, V], U8, name=f"h_scale{o}", align_bytes=64) for o in range(PASSES)]
         x_codes = [keep.tile([P, S], U32, name=f"x_codes{o}", align_bytes=64) for o in range(PASSES)]
         acc = [psum.tile([P, S], F32, name=f"acc{i}") for i in range(TILES)]
-        for o in range(PASSES):
+
+        def quantize_h(o, tag):
+            h_codes[o] = keep.tile([P, V], U32, name=f"h_codes{o}", tag=tag, align_bytes=64)
             nc.vector.quantize_mx(
                 out=h_codes[o][:].bitcast(FP8X4),
                 scales=h_scale[o][:],
                 in_=h_bf[o][:].rearrange("p w j -> p (w j)"),
             )
-        for o in range(PASSES):
+
+        def gather_words(o):
             nc.vector.tensor_copy(x_codes[o][:], word_table[o][:].indirect(offsets[:]))
+
+        def multiply(o):
             for i in range(TILES):
                 cols = slice(i * P, (i + 1) * P)
                 nc.tensor.matmul_mx(
@@ -139,6 +147,15 @@ def tile_picked_ysgm_cost_p_kernel(tc, x_words, x_scales, hT, prev, jump, offs, 
                     start=(o == 0),
                     stop=(o == PASSES - 1),
                 )
+
+        quantize_h(0, "h_codes0")
+        gather_words(0)
+        multiply(0)
+        quantize_h(1, "late0")
+        or_jump(2, "h_bf1")
+        gather_words(1)
+        multiply(1)
+        or_jump(3, "late1")
 
         for i in range(TILES):
             result = keep.tile([P, S], F32, name=f"result{i}")

@@ -1,6 +1,7 @@
 from contextlib import ExitStack
 
 import concourse.mybir as mybir
+from concourse.masks import make_identity
 
 K, T, S, V = 1024, 2048, 512, 512
 FLOPS = 2 * K * V * S
@@ -33,7 +34,8 @@ def tile_picked_ysgm_cost_p_kernel(tc, x_words, x_scales, hT, prev, jump, offs, 
         offsets = keep.tile([P, S // 16], U16, name="offsets")
         scale_table = keep.tile([P, T], U8, name="scale_table", align_bytes=64)
         prev_sb = [keep.tile([P, PAD + S + PAD], F32, name=f"prev{i}") for i in range(TILES)]
-        jump_sb = keep.tile([P, S], F32, name="jump_sb")
+        jump_cols = keep.tile([P, PACK], F32, name="jump_cols")
+        identity = keep.tile([P, P], F32, name="identity")
         h_raw = [keep.tile([P, PACK, V], F32, name=f"h_raw{o}") for o in range(PASSES)]
         word_table = [keep.tile([P, T], U32, name=f"word_table{o}", tag=f"late{o}", align_bytes=64) for o in range(PASSES)]
 
@@ -42,13 +44,16 @@ def tile_picked_ysgm_cost_p_kernel(tc, x_words, x_scales, hT, prev, jump, offs, 
             nc.gpsimd.memset(prev_sb[i][:, 0:PAD], F32_MAX)
             nc.gpsimd.memset(prev_sb[i][:, PAD + S :], F32_MAX)
 
+        make_identity(nc, identity[:])
+
         def load_h(o):
             rows = hT[o * K_PASS : (o + 1) * K_PASS, :]
             nc.sync.dma_start(out=h_raw[o][:], in_=rows.rearrange("(p j) w -> p j w", j=PACK))
 
         for i in range(TILES):
             nc.sync.dma_start(out=prev_sb[i][:, PAD : PAD + S], in_=prev[i * P : (i + 1) * P, :])
-        nc.sync.dma_start(out=jump_sb[:], in_=jump)
+            if i == 0:
+                nc.sync.dma_start(out=jump_cols[:], in_=jump[0].rearrange("(p b) -> p b", b=PACK))
         load_h(0)
         nc.sync.dma_start(offsets[:], offs)
         for q in range(4):
@@ -64,17 +69,25 @@ def tile_picked_ysgm_cost_p_kernel(tc, x_words, x_scales, hT, prev, jump, offs, 
             )
 
         prev1 = [keep.tile([P, S], F32, name=f"prev1_{i}") for i in range(TILES)]
+        jump_rows = psum.tile([P, PACK, P], F32, name="jump_rows")
+        for b in range(PACK):
+            nc.tensor.transpose(jump_rows[:, b, :], jump_cols[:, b : b + 1].to_broadcast([P, P]), identity[:])
+        jump1 = keep.tile([P, S], F32, name="jump1")
         for i in range(TILES):
             nc.scalar.activation(prev1[i][:], prev_sb[i][:, PAD : PAD + S], COPY, bias=1.0)
-        jump1 = keep.tile([P, S], F32, name="jump1")
-        nc.scalar.activation(jump1[:], jump_sb[:], COPY, bias=1.0)
-        nc.gpsimd.tensor_scalar(jump1[:, 0 : S : S - 1], jump1[:, 0 : S : S - 1], 6.3, None, op0=ALU.min)
+            if i == 1:
+                nc.scalar.activation(
+                    jump1[:].rearrange("m (p b) -> m p b", b=PACK),
+                    jump_rows[:].rearrange("m b p -> m p b"),
+                    COPY,
+                    bias=1.0,
+                )
 
         h_bf = [keep.tile([P, V, PACK], BF16, name=f"h_bf{o}", tag=f"h_bf{o}", align_bytes=64) for o in range(PASSES)]
         for o in range(PASSES):
             nc.scalar.copy(
-                out=h_bf[o][:].rearrange("p (c i) t -> p c t i", i=4),
-                in_=h_raw[o][:].rearrange("p t (c i) -> p c t i", i=4),
+                out=h_bf[o][:],
+                in_=h_raw[o][:].rearrange("p t w -> p w t"),
             )
 
         near = [keep.tile([P, 2, S], F32, name=f"near{u}") for u in range(TILES // 2)]
@@ -113,6 +126,7 @@ def tile_picked_ysgm_cost_p_kernel(tc, x_words, x_scales, hT, prev, jump, offs, 
             row_least(u)
             stay_or_step(b)
             if u == 0:
+                nc.vector.tensor_scalar(jump1[:, 0 : S : S - 1], jump1[:, 0 : S : S - 1], 6.3, None, op0=ALU.min)
                 or_jump(a, "path0")
                 or_jump(b, "path1")
 
@@ -158,6 +172,10 @@ def tile_picked_ysgm_cost_p_kernel(tc, x_words, x_scales, hT, prev, jump, offs, 
         or_jump(3, "late1")
 
         for i in range(TILES):
-            result = keep.tile([P, S], F32, name=f"result{i}")
-            nc.vector.scalar_tensor_tensor(result[:], acc[i][:], -0.3, path[i][:], ALU.mult, ALU.add)
-            nc.sync.dma_start(out=out[i * P : (i + 1) * P, :], in_=result[:])
+            pieces = 2 if i == TILES - 1 else 1
+            width = S // pieces
+            for c in range(pieces):
+                cols = slice(c * width, (c + 1) * width)
+                result = keep.tile([P, width], F32, name=f"result{i}_{c}")
+                nc.vector.scalar_tensor_tensor(result[:], acc[i][:, cols], -0.3, path[i][:, cols], ALU.mult, ALU.add)
+                nc.sync.dma_start(out=out[i * P : (i + 1) * P, cols], in_=result[:])

from contextlib import ExitStack

import concourse.mybir as mybir
from concourse.masks import make_identity

K, T, S, V = 1024, 2048, 512, 512
FLOPS = 2 * K * V * S

F32 = mybir.dt.float32
BF16 = mybir.dt.bfloat16
I32 = mybir.dt.int32
U32 = mybir.dt.uint32
U16 = mybir.dt.uint16
U8 = mybir.dt.uint8
FP8X4 = mybir.dt.float8_e4m3fn_x4
ALU = mybir.AluOpType
COPY = mybir.ActivationFunctionType.Copy

P = 128
PACK = 4
K_PASS = P * PACK
PASSES = K // K_PASS
TILES = V // P
PAD = 8
F32_MAX = 3.4028234663852886e38


def tile_picked_ysgm_cost_p_kernel(tc, x_words, x_scales, hT, prev, jump, offs, out):
    nc = tc.nc
    with ExitStack() as ctx:
        keep = ctx.enter_context(tc.tile_pool(name="keep", bufs=1))
        psum = ctx.enter_context(tc.psum_pool(name="psum", bufs=1))

        offsets = keep.tile([P, S // 16], U16, name="offsets")
        scale_table = keep.tile([P, T], U8, name="scale_table", align_bytes=64)
        prev_sb = [keep.tile([P, PAD + S + PAD], F32, name=f"prev{i}") for i in range(TILES)]
        jump_cols = keep.tile([P, PACK], F32, name="jump_cols")
        identity = keep.tile([P, P], F32, name="identity")
        h_raw = [keep.tile([P, PACK, V], F32, name=f"h_raw{o}") for o in range(PASSES)]
        word_table = [keep.tile([P, T], U32, name=f"word_table{o}", tag=f"late{o}", align_bytes=64) for o in range(PASSES)]

        nc.vector.memset(scale_table[:].bitcast(I32), 0)
        for i in range(TILES):
            nc.gpsimd.memset(prev_sb[i][:, 0:PAD], F32_MAX)
            nc.gpsimd.memset(prev_sb[i][:, PAD + S :], F32_MAX)

        make_identity(nc, identity[:])

        def load_h(o):
            rows = hT[o * K_PASS : (o + 1) * K_PASS, :]
            nc.sync.dma_start(out=h_raw[o][:], in_=rows.rearrange("(p j) w -> p j w", j=PACK))

        for i in range(TILES):
            nc.sync.dma_start(out=prev_sb[i][:, PAD : PAD + S], in_=prev[i * P : (i + 1) * P, :])
            if i == 0:
                nc.sync.dma_start(out=jump_cols[:], in_=jump[0].rearrange("(p b) -> p b", b=PACK))
        load_h(0)
        nc.sync.dma_start(offsets[:], offs)
        for q in range(4):
            nc.sync.dma_start(
                out=scale_table[32 * q : 32 * q + 4 * PASSES, :].bitcast(I32),
                in_=x_scales[:, 4 * q : 4 * q + 4, :].bitcast(I32),
            )
        load_h(1)
        for o in range(PASSES):
            nc.sync.dma_start(
                out=word_table[o][:].bitcast(I32),
                in_=x_words[o].rearrange("p c r -> p (c r)").bitcast(I32),
            )

        prev1 = [keep.tile([P, S], F32, name=f"prev1_{i}") for i in range(TILES)]
        jump_rows = psum.tile([P, PACK, P], F32, name="jump_rows")
        for b in range(PACK):
            nc.tensor.transpose(jump_rows[:, b, :], jump_cols[:, b : b + 1].to_broadcast([P, P]), identity[:])
        jump1 = keep.tile([P, S], F32, name="jump1")
        for i in range(TILES):
            nc.scalar.activation(prev1[i][:], prev_sb[i][:, PAD : PAD + S], COPY, bias=1.0)
            if i == 1:
                nc.scalar.activation(
                    jump1[:].rearrange("m (p b) -> m p b", b=PACK),
                    jump_rows[:].rearrange("m b p -> m p b"),
                    COPY,
                    bias=1.0,
                )

        h_bf = [keep.tile([P, V, PACK], BF16, name=f"h_bf{o}", tag=f"h_bf{o}", align_bytes=64) for o in range(PASSES)]
        for o in range(PASSES):
            nc.scalar.copy(
                out=h_bf[o][:],
                in_=h_raw[o][:].rearrange("p t w -> p w t"),
            )

        near = [keep.tile([P, 2, S], F32, name=f"near{u}") for u in range(TILES // 2)]
        least = [keep.tile([P, 2], F32, name=f"least{u}") for u in range(TILES // 2)]
        best = [keep.tile([P, S], F32, name=f"best{i}") for i in range(TILES)]
        path = {}

        def neighbours(i):
            nc.vector.tensor_tensor(
                near[i // 2][:, i % 2, :],
                prev_sb[i][:, PAD - 1 : PAD - 1 + S],
                prev_sb[i][:, PAD + 1 : PAD + 1 + S],
                ALU.min,
            )

        def row_least(u):
            view = near[u][:].rearrange("p e (c f) -> p e c f", f=4)[:, :, :, 1:3]
            nc.vector.tensor_reduce(least[u][:], view, mybir.AxisListType.XY, ALU.min)

        def stay_or_step(i):
            nc.vector.scalar_tensor_tensor(
                best[i][:], near[i // 2][:, i % 2, :], 1.3, prev1[i][:], ALU.add, ALU.min
            )

        def or_jump(i, tag):
            path[i] = keep.tile([P, S], F32, name=f"path{i}", tag=tag, align_bytes=64)
            nc.vector.scalar_tensor_tensor(
                path[i][:], best[i][:], least[i // 2][:, i % 2 : i % 2 + 1], jump1[:], ALU.subtract, ALU.min
            )

        for u in range(TILES // 2):
            a, b = 2 * u, 2 * u + 1
            neighbours(a)
            neighbours(b)
            stay_or_step(a)
            row_least(u)
            stay_or_step(b)
            if u == 0:
                nc.vector.tensor_scalar(jump1[:, 0 : S : S - 1], jump1[:, 0 : S : S - 1], 6.3, None, op0=ALU.min)
                or_jump(a, "path0")
                or_jump(b, "path1")

        x_scale = keep.tile([P, S], U8, name="x_scale", align_bytes=64)
        nc.vector.tensor_copy(x_scale[:], scale_table[:].indirect(offsets[:]))

        h_codes = {}
        h_scale = [keep.tile([P, V], U8, name=f"h_scale{o}", align_bytes=64) for o in range(PASSES)]
        x_codes = [keep.tile([P, S], U32, name=f"x_codes{o}", align_bytes=64) for o in range(PASSES)]
        acc = [psum.tile([P, S], F32, name=f"acc{i}") for i in range(TILES)]

        def quantize_h(o, tag):
            h_codes[o] = keep.tile([P, V], U32, name=f"h_codes{o}", tag=tag, align_bytes=64)
            nc.vector.quantize_mx(
                out=h_codes[o][:].bitcast(FP8X4),
                scales=h_scale[o][:],
                in_=h_bf[o][:].rearrange("p w j -> p (w j)"),
            )

        def gather_words(o):
            nc.vector.tensor_copy(x_codes[o][:], word_table[o][:].indirect(offsets[:]))

        def multiply(o):
            for i in range(TILES):
                cols = slice(i * P, (i + 1) * P)
                nc.tensor.matmul_mx(
                    out=acc[i][:],
                    lhsT=h_codes[o][:, cols].bitcast(FP8X4),
                    lhsT_scale=h_scale[o][:, cols],
                    rhs=x_codes[o][:].bitcast(FP8X4),
                    rhs_scale=x_scale[4 * o : P, :],
                    start=(o == 0),
                    stop=(o == PASSES - 1),
                )

        quantize_h(0, "h_codes0")
        gather_words(0)
        multiply(0)
        quantize_h(1, "late0")
        or_jump(2, "h_bf1")
        gather_words(1)
        multiply(1)
        or_jump(3, "late1")

        for i in range(TILES):
            pieces = 2 if i == TILES - 1 else 1
            width = S // pieces
            for c in range(pieces):
                cols = slice(c * width, (c + 1) * width)
                result = keep.tile([P, width], F32, name=f"result{i}_{c}")
                nc.vector.scalar_tensor_tensor(result[:], acc[i][:, cols], -0.3, path[i][:, cols], ALU.mult, ALU.add)
                nc.sync.dma_start(out=out[i * P : (i + 1) * P, cols], in_=result[:])
